import numpy as np
import ml_dtypes


def mxq(x, axis, fmt="e4m3"):
    dtype, down = {"e4m3": (ml_dtypes.float8_e4m3fn, 7), "e5m2": (ml_dtypes.float8_e5m2, 14)}[fmt]
    v = np.moveaxis(np.asarray(x, np.float32).astype(ml_dtypes.bfloat16).astype(np.float64), axis, -1)
    blocks = v.reshape(v.shape[:-1] + (-1, 32))
    amax = np.abs(blocks).max(-1, keepdims=True)
    byte = np.maximum(np.where(amax > 0, np.frexp(amax)[1] - 1 + 127, 0) - down, 1)
    scale = np.exp2(byte - 127.0)
    codes = (blocks / scale).astype(np.float32).astype(dtype).astype(np.float64)
    return np.moveaxis((codes * scale).reshape(v.shape), -1, axis)


WIDE = False


def mx_kscale(k):
    if not WIDE:
        return np.ones(k)
    levels = np.array([10, -10, 5, -5, 0])
    if k % 512:
        return np.exp2(np.random.permutation(np.resize(levels, k // 32))).repeat(32)
    a = np.empty((k // 512, 16))
    for p in range(k // 512):
        a[p, :8] = np.random.permutation(np.resize(levels, 8))
        for g in range(8):
            far = levels[np.abs(levels - a[p, g]) >= 10]
            a[p, g + 8] = far[np.random.randint(len(far))]
    return np.exp2(a.ravel()).repeat(32)


def f64(x):
    return np.asarray(x).astype(np.float64)


def striped(idx):
    return np.tile(idx.reshape(-1, 16).T, (8, 1)).astype(np.uint16)


def unstriped(offs):
    return offs[:16].T.reshape(-1).astype(np.int64)


def pack_weight(w):
    k, n = w.shape
    w = f64(np.asarray(w, np.float32).astype(ml_dtypes.bfloat16)).reshape(k // 32, 32, n)
    amax = np.abs(w).max(1)
    byte = np.clip(np.where(amax > 0, np.frexp(amax)[1] - 1 + 127 - 7, 1), 1, 254)
    scaled = (w * np.exp2(127.0 - byte)[:, None, :]).reshape(k, n).astype(np.float32)
    words = np.ascontiguousarray(scaled.reshape(k // 512, 128, 4, n).transpose(0, 1, 3, 2)).astype(ml_dtypes.float8_e4m3fn).view(np.uint8)
    return words, np.ascontiguousarray(byte.astype(np.uint8).reshape(k // 512, 16, n))


def unpack_weight(words, scales):
    g, p, n, _ = words.shape
    vals = np.ascontiguousarray(words).view(ml_dtypes.float8_e4m3fn).astype(np.float64) * np.repeat(np.exp2(scales.astype(np.float64) - 127.0), 8, axis=1)[..., None]
    return vals.transpose(0, 1, 3, 2).reshape(g * 512, n)


def sigmoid(v):
    return 1.0 / (1.0 + np.exp(-np.maximum(v, -700.0)))


K, T, S, N = 512, 2048, 1024, 256


def setup_inputs():
    n = np.random.standard_normal
    s = mx_kscale(K)[:, None]
    packed_xT = pack_weight(n((K, T)) * s)
    return {
        "x_words": packed_xT[0],
        "x_scales": packed_xT[1],
        "w1": (n((K, N)) / np.sqrt(K) / s).astype(np.float32),
        "bias": (-np.random.uniform(0.5, 1.5, (N, 1))).astype(np.float32),
        "goal": ((np.random.uniform(size=(N, S)) < 0.2) * np.random.uniform(0.5, 1.0, (N, S))).astype(np.float32),
        "offs": striped(np.random.permutation(T)[:S]),
    }


def reference(x_words, x_scales, w1, bias, goal, offs):
    xq = unpack_weight(x_words, x_scales)[:, unstriped(offs)]
    y = (mxq(f64(w1), 0, "e4m3").T @ xq) + f64(bias)
    p = sigmoid(y)
    ce = np.log(np.exp(y) + 1.0) - (f64(goal) * y)
    return ((f64(goal) - p) ** 2) * ce

@@ -1,0 +1,146 @@
+from contextlib import ExitStack
+
+import concourse.mybir as mybir
+
+K, T, S, N = 512, 2048, 1024, 256
+FLOPS = 2 * K * N * S
+
+F32 = mybir.dt.float32
+BF16 = mybir.dt.bfloat16
+I32 = mybir.dt.int32
+U32 = mybir.dt.uint32
+U16 = mybir.dt.uint16
+U8 = mybir.dt.uint8
+FP8X4 = mybir.dt.float8_e4m3fn_x4
+ALU = mybir.AluOpType
+ACT = mybir.ActivationFunctionType
+
+P = 128
+PACK = 4
+HALVES = N // P
+BANK = 512
+SLICE = 256
+LIST_ROWS = 16
+TINY = 2.0 ** -40
+KNEE = 16.0
+
+
+def tile_picked_yfocal_qfl_p_kernel(tc, x_words, x_scales, w1, bias, goal, offs, out):
+    nc = tc.nc
+    with ExitStack() as ctx:
+        keep = ctx.enter_context(tc.tile_pool(name="keep", bufs=1))
+        psum = ctx.enter_context(tc.psum_pool(name="psum", bufs=1))
+
+        offsets = keep.tile([P, S // LIST_ROWS], U16, name="offsets")
+        nc.sync.dma_start(offsets[:], offs)
+
+        scale_table = keep.tile([P, T], U8, name="scale_table", align_bytes=64)
+        nc.vector.memset(scale_table[:].bitcast(I32), 0)
+        for r in range(4):
+            nc.scalar.dma_start(scale_table[r:P:32, :].bitcast(I32), x_scales[0, r:16:4, :].bitcast(I32))
+
+        w_raw = keep.tile([P, PACK, N], F32, name="w_raw", tag="staging")
+        nc.sync.dma_start(w_raw[:], w1.rearrange("(p j) n -> p j n", j=PACK))
+
+        word_table = keep.tile([P, T], I32, name="word_table", align_bytes=64)
+        nc.sync.dma_start(word_table[:], x_words[0].rearrange("p n t -> p (n t)").bitcast(I32))
+
+        bias_cols = keep.tile([P, HALVES], F32, name="bias_cols")
+        with nc.allow_non_contiguous_dma(reason="one bias value a partition"):
+            nc.sync.dma_start(bias_cols[:], bias.rearrange("(h p) o -> p (h o)", p=P))
+
+        units = [(h, b) for b in range(S // BANK) for h in range(HALVES)]
+
+        warm = keep.tile([P, 1], F32, name="warm")
+        warm_out = keep.tile([P, 1], F32, name="warm_out")
+        nc.vector.memset(warm[:], 0.0)
+        nc.scalar.activation(warm_out[:], warm[:], ACT.Sigmoid)
+
+        scales = keep.tile([P, S], U8, name="scales", align_bytes=64)
+        for b in range(S // BANK):
+            nc.vector.tensor_copy(
+                scales[:, b * BANK : (b + 1) * BANK],
+                scale_table[:].indirect(offsets[:, b * BANK // LIST_ROWS : (b + 1) * BANK // LIST_ROWS]),
+            )
+
+        w_grouped = keep.tile([P, N, PACK], BF16, name="w_grouped", align_bytes=64)
+        nc.scalar.activation(
+            w_grouped[:].rearrange("p (c i) j -> p c j i", i=4),
+            w_raw[:].rearrange("p j (c i) -> p c j i", i=4),
+            ACT.Copy,
+        )
+        w_codes = keep.tile([P, N], U32, name="w_codes", align_bytes=64)
+        w_scales = keep.tile([P, N], U8, name="w_scales", align_bytes=64)
+        nc.vector.quantize_mx(w_codes[:].bitcast(FP8X4), w_scales[:], w_grouped[:].rearrange("p n j -> p (n j)"))
+
+        goal_all = keep.tile([P, len(units) * BANK], F32, name="goal_all", tag="staging")
+        goals = {u: goal_all[:, i * BANK : (i + 1) * BANK] for i, u in enumerate(units)}
+        for b in range(S // BANK):
+            nc.sync.dma_start(
+                goal_all[:, b * HALVES * BANK : (b + 1) * HALVES * BANK].rearrange("p (h s) -> p h s", h=HALVES),
+                goal[:, b * BANK : (b + 1) * BANK].rearrange("(h p) s -> p h s", p=P),
+            )
+
+        knee = keep.tile([P, HALVES], F32, name="knee")
+        nc.gpsimd.tensor_scalar(knee[:], bias_cols[:], -1.0, -KNEE, ALU.mult, ALU.add)
+
+        acc = {u: psum.tile([P, BANK], F32, name=f"acc{u[0]}{u[1]}") for u in units}
+        sig = {u: keep.tile([P, BANK], F32, name=f"sig{u[0]}{u[1]}") for u in units}
+        for part in range(BANK // SLICE):
+            for b in range(S // BANK):
+                first = b * BANK + part * SLICE
+                words = keep.tile([P, SLICE], U32, name=f"words{b}{part}", align_bytes=64)
+                nc.vector.tensor_copy(
+                    words[:],
+                    word_table[:].bitcast(U32).indirect(offsets[:, first // LIST_ROWS : (first + SLICE) // LIST_ROWS]),
+                )
+                cols = slice(part * SLICE, (part + 1) * SLICE)
+                for h in range(HALVES):
+                    nc.tensor.matmul_mx(
+                        acc[h, b][:, cols],
+                        lhsT=w_codes[:, h * P : (h + 1) * P].bitcast(FP8X4),
+                        lhsT_scale=w_scales[:, h * P : (h + 1) * P],
+                        rhs=words[:].bitcast(FP8X4),
+                        rhs_scale=scales[:, first : first + SLICE],
+                        start=True,
+                        stop=True,
+                    )
+                    nc.scalar.activation(sig[h, b][:, cols], acc[h, b][:, cols], ACT.Sigmoid, bias=bias_cols[:, h : h + 1])
+
+        zg, logs, low, diff, sq = {}, {}, {}, {}, {}
+        for u in units:
+            h = u[0]
+            zg[u] = keep.tile([P, BANK], F32, name=f"zg{u[0]}{u[1]}")
+            nc.vector.scalar_tensor_tensor(zg[u][:], acc[u][:], bias_cols[:, h : h + 1], goals[u], ALU.add, ALU.mult)
+            diff[u] = keep.tile([P, BANK], F32, name=f"diff{u[0]}{u[1]}")
+            nc.gpsimd.tensor_tensor(diff[u][:], goals[u], sig[u][:], ALU.subtract)
+        for u in units:
+            h = u[0]
+            low[u] = keep.tile([P, BANK], F32, name=f"low{u[0]}{u[1]}")
+            nc.vector.scalar_tensor_tensor(low[u][:], acc[u][:], knee[:, h : h + 1], zg[u][:], ALU.max, ALU.subtract)
+        for u in units:
+            logs[u] = keep.tile([P, BANK], F32, name=f"logs{u[0]}{u[1]}")
+            nc.scalar.activation(logs[u][:], sig[u][:], ACT.Ln, bias=TINY)
+        for u in units:
+            sq[u] = keep.tile([P, BANK], F32, name=f"sq{u[0]}{u[1]}")
+            nc.scalar.activation(sq[u][:], diff[u][:], ACT.Square)
+
+        ce = {}
+
+        def cross_entropy(u):
+            ce[u] = keep.tile([P, BANK], F32, name=f"ce{u[0]}{u[1]}")
+            nc.vector.scalar_tensor_tensor(ce[u][:], logs[u][:], -KNEE, low[u][:], ALU.max, ALU.subtract, reverse1=True)
+
+        def finish(u, width):
+            h, b = u
+            for c in range(0, BANK, width):
+                cols = slice(c, c + width)
+                loss = keep.tile([P, width], F32, name=f"loss{h}{b}{c}")
+                nc.vector.scalar_tensor_tensor(loss[:], ce[u][:, cols], bias_cols[:, h : h + 1], sq[u][:, cols], ALU.add, ALU.mult)
+                nc.sync.dma_start(out[h * P : (h + 1) * P, b * BANK + c : b * BANK + c + width], loss[:])
+
+        cross_entropy(units[0])
+        for i in range(1, len(units)):
+            cross_entropy(units[i])
+            finish(units[i - 1], BANK)
+        finish(units[-1], SLICE)

@@ -34,13 +34,17 @@ def tile_picked_yfocal_qfl_p_kernel(tc, x_words, x_scales, w1, bias, goal, offs,
         offsets = keep.tile([P, S // LIST_ROWS], U16, name="offsets")
         nc.sync.dma_start(offsets[:], offs)
 
-        scale_table = keep.tile([P, T], U8, name="scale_table", align_bytes=64)
-        nc.vector.memset(scale_table[:].bitcast(I32), 0)
-        for r in range(4):
-            nc.scalar.dma_start(scale_table[r:P:32, :].bitcast(I32), x_scales[0, r:16:4, :].bitcast(I32))
+        w_raw = keep.tile([P, PACK, N], F32, name="w_raw")
+        w_rows = w1.rearrange("(p j) n -> p j n", j=PACK)
+        for j in range(0, PACK, 2):
+            nc.sync.dma_start(w_raw[:, j : j + 2, :], w_rows[:, j : j + 2, :])
 
-        w_raw = keep.tile([P, PACK, N], F32, name="w_raw", tag="staging")
-        nc.sync.dma_start(w_raw[:], w1.rearrange("(p j) n -> p j n", j=PACK))
+        scale_table = keep.tile([P, T], U8, name="scale_table", tag="scale_bytes", align_bytes=64)
+        as_words = scale_table[:].bitcast(I32)
+        nc.vector.memset(as_words[:, : T // 8], 0)
+        nc.gpsimd.memset(as_words[:, T // 8 :], 0)
+        for r in range(4):
+            nc.sync.dma_start(scale_table[r:P:32, :].bitcast(I32), x_scales[0, r:16:4, :].bitcast(I32))
 
         word_table = keep.tile([P, T], I32, name="word_table", align_bytes=64)
         nc.sync.dma_start(word_table[:], x_words[0].rearrange("p n t -> p (n t)").bitcast(I32))
@@ -50,6 +54,12 @@ def tile_picked_yfocal_qfl_p_kernel(tc, x_words, x_scales, w1, bias, goal, offs,
             nc.sync.dma_start(bias_cols[:], bias.rearrange("(h p) o -> p (h o)", p=P))
 
         units = [(h, b) for b in range(S // BANK) for h in range(HALVES)]
+        goals = {}
+        for b in range(S // BANK):
+            goal_part = keep.tile([P, HALVES, BANK], F32, name=f"goal{b}")
+            nc.sync.dma_start(goal_part[:], goal[:, b * BANK : (b + 1) * BANK].rearrange("(h p) s -> p h s", p=P))
+            for h in range(HALVES):
+                goals[h, b] = goal_part[:, h, :]
 
         warm = keep.tile([P, 1], F32, name="warm")
         warm_out = keep.tile([P, 1], F32, name="warm_out")
@@ -57,11 +67,7 @@ def tile_picked_yfocal_qfl_p_kernel(tc, x_words, x_scales, w1, bias, goal, offs,
         nc.scalar.activation(warm_out[:], warm[:], ACT.Sigmoid)
 
         scales = keep.tile([P, S], U8, name="scales", align_bytes=64)
-        for b in range(S // BANK):
-            nc.vector.tensor_copy(
-                scales[:, b * BANK : (b + 1) * BANK],
-                scale_table[:].indirect(offsets[:, b * BANK // LIST_ROWS : (b + 1) * BANK // LIST_ROWS]),
-            )
+        nc.vector.tensor_copy(scales[:], scale_table[:].indirect(offsets[:]))
 
         w_grouped = keep.tile([P, N, PACK], BF16, name="w_grouped", align_bytes=64)
         nc.scalar.activation(
@@ -69,35 +75,24 @@ def tile_picked_yfocal_qfl_p_kernel(tc, x_words, x_scales, w1, bias, goal, offs,
             w_raw[:].rearrange("p j (c i) -> p c j i", i=4),
             ACT.Copy,
         )
-        w_codes = keep.tile([P, N], U32, name="w_codes", align_bytes=64)
+        w_codes = keep.tile([P, N], U32, name="w_codes", tag="scale_bytes", align_bytes=64)
         w_scales = keep.tile([P, N], U8, name="w_scales", align_bytes=64)
         nc.vector.quantize_mx(w_codes[:].bitcast(FP8X4), w_scales[:], w_grouped[:].rearrange("p n j -> p (n j)"))
-
-        goal_all = keep.tile([P, len(units) * BANK], F32, name="goal_all", tag="staging")
-        goals = {u: goal_all[:, i * BANK : (i + 1) * BANK] for i, u in enumerate(units)}
-        for b in range(S // BANK):
-            nc.sync.dma_start(
-                goal_all[:, b * HALVES * BANK : (b + 1) * HALVES * BANK].rearrange("p (h s) -> p h s", h=HALVES),
-                goal[:, b * BANK : (b + 1) * BANK].rearrange("(h p) s -> p h s", p=P),
-            )
 
         knee = keep.tile([P, HALVES], F32, name="knee")
         nc.gpsimd.tensor_scalar(knee[:], bias_cols[:], -1.0, -KNEE, ALU.mult, ALU.add)
 
         acc = {u: psum.tile([P, BANK], F32, name=f"acc{u[0]}{u[1]}") for u in units}
         sig = {u: keep.tile([P, BANK], F32, name=f"sig{u[0]}{u[1]}") for u in units}
-        for part in range(BANK // SLICE):
-            for b in range(S // BANK):
-                first = b * BANK + part * SLICE
-                words = keep.tile([P, SLICE], U32, name=f"words{b}{part}", align_bytes=64)
-                nc.vector.tensor_copy(
-                    words[:],
-                    word_table[:].bitcast(U32).indirect(offsets[:, first // LIST_ROWS : (first + SLICE) // LIST_ROWS]),
-                )
-                cols = slice(part * SLICE, (part + 1) * SLICE)
+        for b in range(S // BANK):
+            for c in range(0, BANK, SLICE):
+                first = b * BANK + c
+                words = keep.tile([P, SLICE], U32, name=f"words{first}", align_bytes=64)
+                entries = offsets[:, first // LIST_ROWS : (first + SLICE) // LIST_ROWS]
+                nc.vector.tensor_copy(words[:], word_table[:].bitcast(U32).indirect(entries))
                 for h in range(HALVES):
                     nc.tensor.matmul_mx(
-                        acc[h, b][:, cols],
+                        acc[h, b][:, c : c + SLICE],
                         lhsT=w_codes[:, h * P : (h + 1) * P].bitcast(FP8X4),
                         lhsT_scale=w_scales[:, h * P : (h + 1) * P],
                         rhs=words[:].bitcast(FP8X4),
@@ -105,34 +100,35 @@ def tile_picked_yfocal_qfl_p_kernel(tc, x_words, x_scales, w1, bias, goal, offs,
                         start=True,
                         stop=True,
                     )
-                    nc.scalar.activation(sig[h, b][:, cols], acc[h, b][:, cols], ACT.Sigmoid, bias=bias_cols[:, h : h + 1])
+            for h in range(HALVES):
+                nc.scalar.activation(sig[h, b][:], acc[h, b][:], ACT.Sigmoid, bias=bias_cols[:, h : h + 1])
 
-        zg, logs, low, diff, sq = {}, {}, {}, {}, {}
-        for u in units:
-            h = u[0]
-            zg[u] = keep.tile([P, BANK], F32, name=f"zg{u[0]}{u[1]}")
-            nc.vector.scalar_tensor_tensor(zg[u][:], acc[u][:], bias_cols[:, h : h + 1], goals[u], ALU.add, ALU.mult)
-            diff[u] = keep.tile([P, BANK], F32, name=f"diff{u[0]}{u[1]}")
-            nc.gpsimd.tensor_tensor(diff[u][:], goals[u], sig[u][:], ALU.subtract)
-        for u in units:
-            h = u[0]
-            low[u] = keep.tile([P, BANK], F32, name=f"low{u[0]}{u[1]}")
-            nc.vector.scalar_tensor_tensor(low[u][:], acc[u][:], knee[:, h : h + 1], zg[u][:], ALU.max, ALU.subtract)
-        for u in units:
-            logs[u] = keep.tile([P, BANK], F32, name=f"logs{u[0]}{u[1]}")
-            nc.scalar.activation(logs[u][:], sig[u][:], ACT.Ln, bias=TINY)
-        for u in units:
-            sq[u] = keep.tile([P, BANK], F32, name=f"sq{u[0]}{u[1]}")
-            nc.scalar.activation(sq[u][:], diff[u][:], ACT.Square)
+        def fresh(kind, u):
+            return keep.tile([P, BANK], F32, name=f"{kind}{u[0]}{u[1]}")
 
-        ce = {}
+        gy, rest, diff, logs, sq, ce = {}, {}, {}, {}, {}, {}
+        for b in range(S // BANK):
+            for h in range(HALVES):
+                u = (h, b)
+                gy[u] = fresh("gy", u)
+                nc.vector.scalar_tensor_tensor(gy[u][:], acc[u][:], bias_cols[:, h : h + 1], goals[u], ALU.add, ALU.mult)
+                diff[u] = fresh("diff", u)
+                nc.gpsimd.tensor_tensor(diff[u][:], goals[u], sig[u][:], ALU.subtract)
+            for h in range(HALVES):
+                u = (h, b)
+                rest[u] = fresh("rest", u)
+                nc.vector.scalar_tensor_tensor(rest[u][:], acc[u][:], knee[:, h : h + 1], gy[u][:], ALU.max, ALU.subtract)
 
         def cross_entropy(u):
-            ce[u] = keep.tile([P, BANK], F32, name=f"ce{u[0]}{u[1]}")
-            nc.vector.scalar_tensor_tensor(ce[u][:], logs[u][:], -KNEE, low[u][:], ALU.max, ALU.subtract, reverse1=True)
+            logs[u] = fresh("logs", u)
+            nc.scalar.activation(logs[u][:], sig[u][:], ACT.Ln, bias=TINY)
+            ce[u] = fresh("ce", u)
+            nc.vector.scalar_tensor_tensor(ce[u][:], logs[u][:], -KNEE, rest[u][:], ALU.max, ALU.subtract, reverse1=True)
 
         def finish(u, width):
             h, b = u
+            sq[u] = fresh("sq", u)
+            nc.scalar.activation(sq[u][:], diff[u][:], ACT.Square)
             for c in range(0, BANK, width):
                 cols = slice(c, c + width)
                 loss = keep.tile([P, width], F32, name=f"loss{h}{b}{c}")
@@ -143,4 +139,4 @@ def tile_picked_yfocal_qfl_p_kernel(tc, x_words, x_scales, w1, bias, goal, offs,
         for i in range(1, len(units)):
             cross_entropy(units[i])
             finish(units[i - 1], BANK)
-        finish(units[-1], SLICE)
+        finish(units[-1], BANK // 2)

@@ -85,22 +85,23 @@ def tile_picked_yfocal_qfl_p_kernel(tc, x_words, x_scales, w1, bias, goal, offs,
         acc = {u: psum.tile([P, BANK], F32, name=f"acc{u[0]}{u[1]}") for u in units}
         sig = {u: keep.tile([P, BANK], F32, name=f"sig{u[0]}{u[1]}") for u in units}
         for b in range(S // BANK):
+            words = {}
             for c in range(0, BANK, SLICE):
                 first = b * BANK + c
-                words = keep.tile([P, SLICE], U32, name=f"words{first}", align_bytes=64)
+                words[c] = keep.tile([P, SLICE], U32, name=f"words{first}", align_bytes=64)
                 entries = offsets[:, first // LIST_ROWS : (first + SLICE) // LIST_ROWS]
-                nc.vector.tensor_copy(words[:], word_table[:].bitcast(U32).indirect(entries))
-                for h in range(HALVES):
+                nc.vector.tensor_copy(words[c][:], word_table[:].bitcast(U32).indirect(entries))
+            for h in range(HALVES):
+                for c in range(0, BANK, SLICE):
                     nc.tensor.matmul_mx(
                         acc[h, b][:, c : c + SLICE],
                         lhsT=w_codes[:, h * P : (h + 1) * P].bitcast(FP8X4),
                         lhsT_scale=w_scales[:, h * P : (h + 1) * P],
-                        rhs=words[:].bitcast(FP8X4),
-                        rhs_scale=scales[:, first : first + SLICE],
+                        rhs=words[c][:].bitcast(FP8X4),
+                        rhs_scale=scales[:, b * BANK + c : b * BANK + c + SLICE],
                         start=True,
                         stop=True,
                     )
-            for h in range(HALVES):
                 nc.scalar.activation(sig[h, b][:], acc[h, b][:], ACT.Sigmoid, bias=bias_cols[:, h : h + 1])
 
         def fresh(kind, u):
@@ -113,7 +114,7 @@ def tile_picked_yfocal_qfl_p_kernel(tc, x_words, x_scales, w1, bias, goal, offs,
                 gy[u] = fresh("gy", u)
                 nc.vector.scalar_tensor_tensor(gy[u][:], acc[u][:], bias_cols[:, h : h + 1], goals[u], ALU.add, ALU.mult)
                 diff[u] = fresh("diff", u)
-                nc.gpsimd.tensor_tensor(diff[u][:], goals[u], sig[u][:], ALU.subtract)
+                nc.vector.tensor_tensor(diff[u][:], goals[u], sig[u][:], ALU.subtract)
             for h in range(HALVES):
                 u = (h, b)
                 rest[u] = fresh("rest", u)

@@ -21,8 +21,9 @@ HALVES = N // P
 BANK = 512
 SLICE = 256
 LIST_ROWS = 16
-TINY = 2.0 ** -40
+FLOOR_LOGIT = -28.0
 KNEE = 16.0
+POOL_LAST = 384
 
 
 def tile_picked_yfocal_qfl_p_kernel(tc, x_words, x_scales, w1, bias, goal, offs, out):
@@ -34,10 +35,10 @@ def tile_picked_yfocal_qfl_p_kernel(tc, x_words, x_scales, w1, bias, goal, offs,
         offsets = keep.tile([P, S // LIST_ROWS], U16, name="offsets")
         nc.sync.dma_start(offsets[:], offs)
 
-        w_raw = keep.tile([P, PACK, N], F32, name="w_raw")
         w_rows = w1.rearrange("(p j) n -> p j n", j=PACK)
+        w_raw = [keep.tile([P, PACK, P], F32, name=f"w_raw{h}") for h in range(HALVES)]
         for j in range(0, PACK, 2):
-            nc.sync.dma_start(w_raw[:, j : j + 2, :], w_rows[:, j : j + 2, :])
+            nc.sync.dma_start(w_raw[0][:, j : j + 2, :], w_rows[:, j : j + 2, :P])
 
         scale_table = keep.tile([P, T], U8, name="scale_table", tag="scale_bytes", align_bytes=64)
         as_words = scale_table[:].bitcast(I32)
@@ -48,6 +49,8 @@ def tile_picked_yfocal_qfl_p_kernel(tc, x_words, x_scales, w1, bias, goal, offs,
 
         word_table = keep.tile([P, T], I32, name="word_table", align_bytes=64)
         nc.sync.dma_start(word_table[:], x_words[0].rearrange("p n t -> p (n t)").bitcast(I32))
+
+        nc.sync.dma_start(w_raw[1][:], w_rows[:, :, P:])
 
         bias_cols = keep.tile([P, HALVES], F32, name="bias_cols")
         with nc.allow_non_contiguous_dma(reason="one bias value a partition"):
@@ -61,83 +64,109 @@ def tile_picked_yfocal_qfl_p_kernel(tc, x_words, x_scales, w1, bias, goal, offs,
             for h in range(HALVES):
                 goals[h, b] = goal_part[:, h, :]
 
-        warm = keep.tile([P, 1], F32, name="warm")
-        warm_out = keep.tile([P, 1], F32, name="warm_out")
-        nc.vector.memset(warm[:], 0.0)
-        nc.scalar.activation(warm_out[:], warm[:], ACT.Sigmoid)
+        floor_logit = keep.tile([P, 1], F32, name="floor_logit")
+        floor = keep.tile([P, 1], F32, name="floor")
+        nc.vector.memset(floor_logit[:], FLOOR_LOGIT)
+        nc.scalar.activation(floor[:], floor_logit[:], ACT.Sigmoid)
 
         scales = keep.tile([P, S], U8, name="scales", align_bytes=64)
         nc.vector.tensor_copy(scales[:], scale_table[:].indirect(offsets[:]))
 
-        w_grouped = keep.tile([P, N, PACK], BF16, name="w_grouped", align_bytes=64)
-        nc.scalar.activation(
-            w_grouped[:].rearrange("p (c i) j -> p c j i", i=4),
-            w_raw[:].rearrange("p j (c i) -> p c j i", i=4),
-            ACT.Copy,
-        )
-        w_codes = keep.tile([P, N], U32, name="w_codes", tag="scale_bytes", align_bytes=64)
-        w_scales = keep.tile([P, N], U8, name="w_scales", align_bytes=64)
-        nc.vector.quantize_mx(w_codes[:].bitcast(FP8X4), w_scales[:], w_grouped[:].rearrange("p n j -> p (n j)"))
+        w_codes, w_scales = [], []
+        for h in range(HALVES):
+            w_grouped = keep.tile([P, P, PACK], BF16, name=f"w_grouped{h}", tag=f"grouped_bytes{h}", align_bytes=64)
+            nc.scalar.activation(
+                w_grouped[:].rearrange("p (c i) j -> p c j i", i=4),
+                w_raw[h][:].rearrange("p j (c i) -> p c j i", i=4),
+                ACT.Copy,
+            )
+            tag = "scale_bytes" if h == 0 else "w_codes1"
+            w_codes.append(keep.tile([P, P], U32, name=f"w_codes{h}", tag=tag, align_bytes=64))
+            w_scales.append(keep.tile([P, P], U8, name=f"w_scales{h}", align_bytes=64))
+            nc.vector.quantize_mx(w_codes[h][:].bitcast(FP8X4), w_scales[h][:], w_grouped[:].rearrange("p n j -> p (n j)"))
 
         knee = keep.tile([P, HALVES], F32, name="knee")
         nc.gpsimd.tensor_scalar(knee[:], bias_cols[:], -1.0, -KNEE, ALU.mult, ALU.add)
 
-        acc = {u: psum.tile([P, BANK], F32, name=f"acc{u[0]}{u[1]}") for u in units}
-        sig = {u: keep.tile([P, BANK], F32, name=f"sig{u[0]}{u[1]}") for u in units}
+        def fresh(kind, u):
+            return keep.tile([P, BANK], F32, name=f"{kind}{u[0]}{u[1]}")
+
+        sig = {u: fresh("sig", u) for u in units}
+        gy = {u: fresh("gy", u) for u in units}
+        rest = {u: fresh("rest", u) for u in units}
+        diff = {u: fresh("diff", u) for u in units}
+        logs, sq, ce = {}, {}, {}
+
+        stretches = [(0, slice(0, BANK))] + [(1, slice(c, c + SLICE)) for c in range(0, BANK, SLICE)]
+        words = []
         for b in range(S // BANK):
-            words = {}
+            tag = "grouped_bytes1" if b == 1 else "words0"
+            words.append(keep.tile([P, BANK], U32, name=f"words{b}", tag=tag, align_bytes=64))
             for c in range(0, BANK, SLICE):
                 first = b * BANK + c
-                words[c] = keep.tile([P, SLICE], U32, name=f"words{first}", align_bytes=64)
                 entries = offsets[:, first // LIST_ROWS : (first + SLICE) // LIST_ROWS]
-                nc.vector.tensor_copy(words[c][:], word_table[:].bitcast(U32).indirect(entries))
+                nc.vector.tensor_copy(words[b][:, c : c + SLICE], word_table[:].bitcast(U32).indirect(entries))
+
+        acc = {}
+        for b, cols in stretches:
             for h in range(HALVES):
-                for c in range(0, BANK, SLICE):
+                sums = psum.tile([P, cols.stop - cols.start], F32, name=f"acc{h}{b}{cols.start}")
+                acc[h, b, cols.start] = sums
+                for c in range(cols.start, cols.stop, SLICE):
                     nc.tensor.matmul_mx(
-                        acc[h, b][:, c : c + SLICE],
-                        lhsT=w_codes[:, h * P : (h + 1) * P].bitcast(FP8X4),
-                        lhsT_scale=w_scales[:, h * P : (h + 1) * P],
-                        rhs=words[c][:].bitcast(FP8X4),
+                        sums[:, c - cols.start : c - cols.start + SLICE],
+                        lhsT=w_codes[h][:].bitcast(FP8X4),
+                        lhsT_scale=w_scales[h][:],
+                        rhs=words[b][:, c : c + SLICE].bitcast(FP8X4),
                         rhs_scale=scales[:, b * BANK + c : b * BANK + c + SLICE],
                         start=True,
                         stop=True,
                     )
-                nc.scalar.activation(sig[h, b][:], acc[h, b][:], ACT.Sigmoid, bias=bias_cols[:, h : h + 1])
+                nc.scalar.activation(sig[h, b][:, cols], sums[:], ACT.Sigmoid, bias=bias_cols[:, h : h + 1])
 
-        def fresh(kind, u):
-            return keep.tile([P, BANK], F32, name=f"{kind}{u[0]}{u[1]}")
-
-        gy, rest, diff, logs, sq, ce = {}, {}, {}, {}, {}, {}
-        for b in range(S // BANK):
+        for b, cols in stretches:
             for h in range(HALVES):
-                u = (h, b)
-                gy[u] = fresh("gy", u)
-                nc.vector.scalar_tensor_tensor(gy[u][:], acc[u][:], bias_cols[:, h : h + 1], goals[u], ALU.add, ALU.mult)
-                diff[u] = fresh("diff", u)
-                nc.vector.tensor_tensor(diff[u][:], goals[u], sig[u][:], ALU.subtract)
+                nc.vector.scalar_tensor_tensor(
+                    gy[h, b][:, cols], acc[h, b, cols.start][:], bias_cols[:, h : h + 1], goals[h, b][:, cols], ALU.add, ALU.mult
+                )
             for h in range(HALVES):
-                u = (h, b)
-                rest[u] = fresh("rest", u)
-                nc.vector.scalar_tensor_tensor(rest[u][:], acc[u][:], knee[:, h : h + 1], gy[u][:], ALU.max, ALU.subtract)
+                nc.vector.scalar_tensor_tensor(
+                    rest[h, b][:, cols], acc[h, b, cols.start][:], knee[:, h : h + 1], gy[h, b][:, cols], ALU.max, ALU.subtract
+                )
+        for u in units:
+            share = POOL_LAST if u == units[-1] else BANK
+            nc.gpsimd.tensor_tensor(diff[u][:, :share], goals[u][:, :share], sig[u][:, :share], ALU.subtract)
 
-        def cross_entropy(u):
+        last = units[-1]
+        nc.vector.tensor_tensor(diff[last][:, POOL_LAST:], goals[last][:, POOL_LAST:], sig[last][:, POOL_LAST:], ALU.subtract)
+
+        def logarithm(u):
             logs[u] = fresh("logs", u)
-            nc.scalar.activation(logs[u][:], sig[u][:], ACT.Ln, bias=TINY)
+            nc.scalar.activation(logs[u][:], sig[u][:], ACT.Ln, bias=floor[:])
             ce[u] = fresh("ce", u)
-            nc.vector.scalar_tensor_tensor(ce[u][:], logs[u][:], -KNEE, rest[u][:], ALU.max, ALU.subtract, reverse1=True)
 
-        def finish(u, width):
-            h, b = u
+        def square(u):
             sq[u] = fresh("sq", u)
             nc.scalar.activation(sq[u][:], diff[u][:], ACT.Square)
-            for c in range(0, BANK, width):
-                cols = slice(c, c + width)
-                loss = keep.tile([P, width], F32, name=f"loss{h}{b}{c}")
-                nc.vector.scalar_tensor_tensor(loss[:], ce[u][:, cols], bias_cols[:, h : h + 1], sq[u][:, cols], ALU.add, ALU.mult)
-                nc.sync.dma_start(out[h * P : (h + 1) * P, b * BANK + c : b * BANK + c + width], loss[:])
 
-        cross_entropy(units[0])
-        for i in range(1, len(units)):
-            cross_entropy(units[i])
-            finish(units[i - 1], BANK)
-        finish(units[-1], BANK // 2)
+        def cross_entropy(u, cols):
+            nc.vector.scalar_tensor_tensor(ce[u][:, cols], logs[u][:, cols], -KNEE, rest[u][:, cols], ALU.max, ALU.subtract, reverse1=True)
+
+        def finish(u, cols):
+            h, b = u
+            loss = keep.tile([P, cols.stop - cols.start], F32, name=f"loss{h}{b}{cols.start}")
+            nc.vector.scalar_tensor_tensor(loss[:], ce[u][:, cols], bias_cols[:, h : h + 1], sq[u][:, cols], ALU.add, ALU.mult)
+            nc.sync.dma_start(out[h * P : (h + 1) * P, b * BANK + cols.start : b * BANK + cols.stop], loss[:])
+
+        pieces = [(u, slice(0, BANK)) for u in units[:-1]] + [(last, slice(c, c + SLICE)) for c in range(0, BANK, SLICE)]
+        for i in range(len(pieces) + 1):
+            if i < len(pieces):
+                u, cols = pieces[i]
+                if cols.start == 0:
+                    logarithm(u)
+                cross_entropy(u, cols)
+            if i > 0:
+                u, cols = pieces[i - 1]
+                if cols.start == 0:
+                    square(u)
+                finish(u, cols)

@@ -17,13 +17,15 @@ ACT = mybir.ActivationFunctionType
 
 P = 128
 PACK = 4
-HALVES = N // P
-BANK = 512
-SLICE = 256
+QUADRANT = 32
+SCALE_ROWS = K // 32
 LIST_ROWS = 16
-FLOOR_LOGIT = -28.0
+HALVES = N // P
+SLICE = 256
+WIDE = 512
 KNEE = 16.0
-POOL_LAST = 384
+FLOOR_LOGIT = -28.0
+GPSIMD_LAST = 320
 
 
 def tile_picked_yfocal_qfl_p_kernel(tc, x_words, x_scales, w1, bias, goal, offs, out):
@@ -31,6 +33,8 @@ def tile_picked_yfocal_qfl_p_kernel(tc, x_words, x_scales, w1, bias, goal, offs,
     with ExitStack() as ctx:
         keep = ctx.enter_context(tc.tile_pool(name="keep", bufs=1))
         psum = ctx.enter_context(tc.psum_pool(name="psum", bufs=1))
+        units = [(h, b) for b in range(S // WIDE) for h in range(HALVES)]
+        last = units[-1]
 
         offsets = keep.tile([P, S // LIST_ROWS], U16, name="offsets")
         nc.sync.dma_start(offsets[:], offs)
@@ -41,11 +45,11 @@ def tile_picked_yfocal_qfl_p_kernel(tc, x_words, x_scales, w1, bias, goal, offs,
             nc.sync.dma_start(w_raw[0][:, j : j + 2, :], w_rows[:, j : j + 2, :P])
 
         scale_table = keep.tile([P, T], U8, name="scale_table", tag="scale_bytes", align_bytes=64)
-        as_words = scale_table[:].bitcast(I32)
-        nc.vector.memset(as_words[:, : T // 8], 0)
-        nc.gpsimd.memset(as_words[:, T // 8 :], 0)
+        to_clear = scale_table[:].bitcast(I32)
+        nc.vector.memset(to_clear[:, : T // 8], 0)
+        nc.gpsimd.memset(to_clear[:, T // 8 :], 0)
         for r in range(4):
-            nc.sync.dma_start(scale_table[r:P:32, :].bitcast(I32), x_scales[0, r:16:4, :].bitcast(I32))
+            nc.sync.dma_start(scale_table[r:P:QUADRANT, :].bitcast(I32), x_scales[0, r:SCALE_ROWS:4, :].bitcast(I32))
 
         word_table = keep.tile([P, T], I32, name="word_table", align_bytes=64)
         nc.sync.dma_start(word_table[:], x_words[0].rearrange("p n t -> p (n t)").bitcast(I32))
@@ -53,16 +57,15 @@ def tile_picked_yfocal_qfl_p_kernel(tc, x_words, x_scales, w1, bias, goal, offs,
         nc.sync.dma_start(w_raw[1][:], w_rows[:, :, P:])
 
         bias_cols = keep.tile([P, HALVES], F32, name="bias_cols")
-        with nc.allow_non_contiguous_dma(reason="one bias value a partition"):
+        with nc.allow_non_contiguous_dma(reason="one bias value a partition and class half"):
             nc.sync.dma_start(bias_cols[:], bias.rearrange("(h p) o -> p (h o)", p=P))
 
-        units = [(h, b) for b in range(S // BANK) for h in range(HALVES)]
-        goals = {}
-        for b in range(S // BANK):
-            goal_part = keep.tile([P, HALVES, BANK], F32, name=f"goal{b}")
-            nc.sync.dma_start(goal_part[:], goal[:, b * BANK : (b + 1) * BANK].rearrange("(h p) s -> p h s", p=P))
-            for h in range(HALVES):
-                goals[h, b] = goal_part[:, h, :]
+        def unit_tiles(kind):
+            return {u: keep.tile([P, WIDE], F32, name=f"{kind}{u[0]}{u[1]}") for u in units}
+
+        goals = unit_tiles("goal")
+        for h, b in units:
+            nc.sync.dma_start(goals[h, b][:], goal[h * P : (h + 1) * P, b * WIDE : (b + 1) * WIDE])
 
         floor_logit = keep.tile([P, 1], F32, name="floor_logit")
         floor = keep.tile([P, 1], F32, name="floor")
@@ -80,93 +83,77 @@ def tile_picked_yfocal_qfl_p_kernel(tc, x_words, x_scales, w1, bias, goal, offs,
                 w_raw[h][:].rearrange("p j (c i) -> p c j i", i=4),
                 ACT.Copy,
             )
-            tag = "scale_bytes" if h == 0 else "w_codes1"
-            w_codes.append(keep.tile([P, P], U32, name=f"w_codes{h}", tag=tag, align_bytes=64))
+            codes_tag = "scale_bytes" if h == 0 else "w_codes1"
+            w_codes.append(keep.tile([P, P], U32, name=f"w_codes{h}", tag=codes_tag, align_bytes=64))
             w_scales.append(keep.tile([P, P], U8, name=f"w_scales{h}", align_bytes=64))
             nc.vector.quantize_mx(w_codes[h][:].bitcast(FP8X4), w_scales[h][:], w_grouped[:].rearrange("p n j -> p (n j)"))
 
-        knee = keep.tile([P, HALVES], F32, name="knee")
-        nc.gpsimd.tensor_scalar(knee[:], bias_cols[:], -1.0, -KNEE, ALU.mult, ALU.add)
+        knee_cols = keep.tile([P, HALVES], F32, name="knee_cols")
+        nc.scalar.activation(knee_cols[:], bias_cols[:], ACT.Copy, bias=-KNEE, scale=-1.0)
 
-        def fresh(kind, u):
-            return keep.tile([P, BANK], F32, name=f"{kind}{u[0]}{u[1]}")
-
-        sig = {u: fresh("sig", u) for u in units}
-        gy = {u: fresh("gy", u) for u in units}
-        rest = {u: fresh("rest", u) for u in units}
-        diff = {u: fresh("diff", u) for u in units}
-        logs, sq, ce = {}, {}, {}
-
-        stretches = [(0, slice(0, BANK))] + [(1, slice(c, c + SLICE)) for c in range(0, BANK, SLICE)]
         words = []
-        for b in range(S // BANK):
-            tag = "grouped_bytes1" if b == 1 else "words0"
-            words.append(keep.tile([P, BANK], U32, name=f"words{b}", tag=tag, align_bytes=64))
-            for c in range(0, BANK, SLICE):
-                first = b * BANK + c
+        for b in range(S // WIDE):
+            words_tag = "grouped_bytes1" if b == 1 else "words0"
+            words.append(keep.tile([P, WIDE], U32, name=f"words{b}", tag=words_tag, align_bytes=64))
+            for c in range(0, WIDE, SLICE):
+                first = b * WIDE + c
                 entries = offsets[:, first // LIST_ROWS : (first + SLICE) // LIST_ROWS]
                 nc.vector.tensor_copy(words[b][:, c : c + SLICE], word_table[:].bitcast(U32).indirect(entries))
 
-        acc = {}
-        for b, cols in stretches:
+        prob, goal_y, linear, miss = (unit_tiles(kind) for kind in ("prob", "goal_y", "linear", "miss"))
+        slices = [(b, slice(c, c + SLICE)) for b in range(S // WIDE) for c in range(0, WIDE, SLICE)]
+        sums = {}
+        for b, cols in slices:
             for h in range(HALVES):
-                sums = psum.tile([P, cols.stop - cols.start], F32, name=f"acc{h}{b}{cols.start}")
-                acc[h, b, cols.start] = sums
-                for c in range(cols.start, cols.stop, SLICE):
-                    nc.tensor.matmul_mx(
-                        sums[:, c - cols.start : c - cols.start + SLICE],
-                        lhsT=w_codes[h][:].bitcast(FP8X4),
-                        lhsT_scale=w_scales[h][:],
-                        rhs=words[b][:, c : c + SLICE].bitcast(FP8X4),
-                        rhs_scale=scales[:, b * BANK + c : b * BANK + c + SLICE],
-                        start=True,
-                        stop=True,
-                    )
-                nc.scalar.activation(sig[h, b][:, cols], sums[:], ACT.Sigmoid, bias=bias_cols[:, h : h + 1])
+                sums[h, b, cols.start] = psum.tile([P, SLICE], F32, name=f"sums{h}{b}{cols.start}")
+                nc.tensor.matmul_mx(
+                    sums[h, b, cols.start][:],
+                    lhsT=w_codes[h][:].bitcast(FP8X4),
+                    lhsT_scale=w_scales[h][:],
+                    rhs=words[b][:, cols].bitcast(FP8X4),
+                    rhs_scale=scales[:, b * WIDE + cols.start : b * WIDE + cols.stop],
+                    start=True,
+                    stop=True,
+                )
+                nc.scalar.activation(prob[h, b][:, cols], sums[h, b, cols.start][:], ACT.Sigmoid, bias=bias_cols[:, h : h + 1])
 
-        for b, cols in stretches:
+        for b, cols in slices:
             for h in range(HALVES):
                 nc.vector.scalar_tensor_tensor(
-                    gy[h, b][:, cols], acc[h, b, cols.start][:], bias_cols[:, h : h + 1], goals[h, b][:, cols], ALU.add, ALU.mult
+                    goal_y[h, b][:, cols], sums[h, b, cols.start][:], bias_cols[:, h : h + 1], goals[h, b][:, cols], ALU.add, ALU.mult
                 )
             for h in range(HALVES):
                 nc.vector.scalar_tensor_tensor(
-                    rest[h, b][:, cols], acc[h, b, cols.start][:], knee[:, h : h + 1], gy[h, b][:, cols], ALU.max, ALU.subtract
+                    linear[h, b][:, cols], sums[h, b, cols.start][:], knee_cols[:, h : h + 1], goal_y[h, b][:, cols], ALU.max, ALU.subtract
                 )
-        for u in units:
-            share = POOL_LAST if u == units[-1] else BANK
-            nc.gpsimd.tensor_tensor(diff[u][:, :share], goals[u][:, :share], sig[u][:, :share], ALU.subtract)
 
-        last = units[-1]
-        nc.vector.tensor_tensor(diff[last][:, POOL_LAST:], goals[last][:, POOL_LAST:], sig[last][:, POOL_LAST:], ALU.subtract)
+        first_unit = [(units[0], slice(c, c + SLICE)) for c in range(0, WIDE, SLICE)]
+        for u, cols in first_unit + [(u, slice(0, WIDE)) for u in units[1:-1]] + [(last, slice(0, GPSIMD_LAST))]:
+            nc.gpsimd.tensor_tensor(miss[u][:, cols], goals[u][:, cols], prob[u][:, cols], ALU.subtract)
+        nc.vector.tensor_tensor(miss[last][:, GPSIMD_LAST:], goals[last][:, GPSIMD_LAST:], prob[last][:, GPSIMD_LAST:], ALU.subtract)
 
-        def logarithm(u):
-            logs[u] = fresh("logs", u)
-            nc.scalar.activation(logs[u][:], sig[u][:], ACT.Ln, bias=floor[:])
-            ce[u] = fresh("ce", u)
-
-        def square(u):
-            sq[u] = fresh("sq", u)
-            nc.scalar.activation(sq[u][:], diff[u][:], ACT.Square)
+        log_prob, weight, ce_less_bias = (unit_tiles(kind) for kind in ("log_prob", "weight", "ce_less_bias"))
 
         def cross_entropy(u, cols):
-            nc.vector.scalar_tensor_tensor(ce[u][:, cols], logs[u][:, cols], -KNEE, rest[u][:, cols], ALU.max, ALU.subtract, reverse1=True)
+            if cols.start == 0:
+                nc.scalar.activation(log_prob[u][:], prob[u][:], ACT.Ln, bias=floor[:])
+            nc.vector.scalar_tensor_tensor(
+                ce_less_bias[u][:, cols], log_prob[u][:, cols], -KNEE, linear[u][:, cols], ALU.max, ALU.subtract, reverse1=True
+            )
 
-        def finish(u, cols):
+        def loss(u, cols):
             h, b = u
-            loss = keep.tile([P, cols.stop - cols.start], F32, name=f"loss{h}{b}{cols.start}")
-            nc.vector.scalar_tensor_tensor(loss[:], ce[u][:, cols], bias_cols[:, h : h + 1], sq[u][:, cols], ALU.add, ALU.mult)
-            nc.sync.dma_start(out[h * P : (h + 1) * P, b * BANK + cols.start : b * BANK + cols.stop], loss[:])
+            if cols.start == 0:
+                nc.scalar.activation(weight[u][:], miss[u][:], ACT.Square)
+            result = keep.tile([P, cols.stop - cols.start], F32, name=f"result{h}{b}{cols.start}")
+            nc.vector.scalar_tensor_tensor(
+                result[:], ce_less_bias[u][:, cols], bias_cols[:, h : h + 1], weight[u][:, cols], ALU.add, ALU.mult
+            )
+            nc.sync.dma_start(out[h * P : (h + 1) * P, b * WIDE + cols.start : b * WIDE + cols.stop], result[:])
 
-        pieces = [(u, slice(0, BANK)) for u in units[:-1]] + [(last, slice(c, c + SLICE)) for c in range(0, BANK, SLICE)]
-        for i in range(len(pieces) + 1):
-            if i < len(pieces):
-                u, cols = pieces[i]
-                if cols.start == 0:
-                    logarithm(u)
-                cross_entropy(u, cols)
-            if i > 0:
-                u, cols = pieces[i - 1]
-                if cols.start == 0:
-                    square(u)
-                finish(u, cols)
+        pieces = [(u, slice(0, WIDE)) for u in units[:-1]] + [(last, slice(c, c + SLICE)) for c in range(0, WIDE, SLICE)]
+        cross_entropy(*pieces[0])
+        for ahead, behind in zip(pieces[1:], pieces):
+            cross_entropy(*ahead)
+            loss(*behind)
+        loss(*pieces[-1])

from contextlib import ExitStack

import concourse.mybir as mybir

K, T, S, N = 512, 2048, 1024, 256
FLOPS = 2 * K * N * S

F32 = mybir.dt.float32
BF16 = mybir.dt.bfloat16
I32 = mybir.dt.int32
U32 = mybir.dt.uint32
U16 = mybir.dt.uint16
U8 = mybir.dt.uint8
FP8X4 = mybir.dt.float8_e4m3fn_x4
ALU = mybir.AluOpType
ACT = mybir.ActivationFunctionType

P = 128
PACK = 4
QUADRANT = 32
SCALE_ROWS = K // 32
LIST_ROWS = 16
HALVES = N // P
SLICE = 256
WIDE = 512
KNEE = 16.0
FLOOR_LOGIT = -28.0
GPSIMD_LAST = 320


def tile_picked_yfocal_qfl_p_kernel(tc, x_words, x_scales, w1, bias, goal, offs, out):
    nc = tc.nc
    with ExitStack() as ctx:
        keep = ctx.enter_context(tc.tile_pool(name="keep", bufs=1))
        psum = ctx.enter_context(tc.psum_pool(name="psum", bufs=1))
        units = [(h, b) for b in range(S // WIDE) for h in range(HALVES)]
        last = units[-1]

        offsets = keep.tile([P, S // LIST_ROWS], U16, name="offsets")
        nc.sync.dma_start(offsets[:], offs)

        w_rows = w1.rearrange("(p j) n -> p j n", j=PACK)
        w_raw = [keep.tile([P, PACK, P], F32, name=f"w_raw{h}") for h in range(HALVES)]
        for j in range(0, PACK, 2):
            nc.sync.dma_start(w_raw[0][:, j : j + 2, :], w_rows[:, j : j + 2, :P])

        scale_table = keep.tile([P, T], U8, name="scale_table", tag="scale_bytes", align_bytes=64)
        to_clear = scale_table[:].bitcast(I32)
        nc.vector.memset(to_clear[:, : T // 8], 0)
        nc.gpsimd.memset(to_clear[:, T // 8 :], 0)
        for r in range(4):
            nc.sync.dma_start(scale_table[r:P:QUADRANT, :].bitcast(I32), x_scales[0, r:SCALE_ROWS:4, :].bitcast(I32))

        word_table = keep.tile([P, T], I32, name="word_table", align_bytes=64)
        nc.sync.dma_start(word_table[:], x_words[0].rearrange("p n t -> p (n t)").bitcast(I32))

        nc.sync.dma_start(w_raw[1][:], w_rows[:, :, P:])

        bias_cols = keep.tile([P, HALVES], F32, name="bias_cols")
        with nc.allow_non_contiguous_dma(reason="one bias value a partition and class half"):
            nc.sync.dma_start(bias_cols[:], bias.rearrange("(h p) o -> p (h o)", p=P))

        def unit_tiles(kind):
            return {u: keep.tile([P, WIDE], F32, name=f"{kind}{u[0]}{u[1]}") for u in units}

        goals = unit_tiles("goal")
        for h, b in units:
            nc.sync.dma_start(goals[h, b][:], goal[h * P : (h + 1) * P, b * WIDE : (b + 1) * WIDE])

        floor_logit = keep.tile([P, 1], F32, name="floor_logit")
        floor = keep.tile([P, 1], F32, name="floor")
        nc.vector.memset(floor_logit[:], FLOOR_LOGIT)
        nc.scalar.activation(floor[:], floor_logit[:], ACT.Sigmoid)

        scales = keep.tile([P, S], U8, name="scales", align_bytes=64)
        nc.vector.tensor_copy(scales[:], scale_table[:].indirect(offsets[:]))

        w_codes, w_scales = [], []
        for h in range(HALVES):
            w_grouped = keep.tile([P, P, PACK], BF16, name=f"w_grouped{h}", tag=f"grouped_bytes{h}", align_bytes=64)
            nc.scalar.activation(
                w_grouped[:].rearrange("p (c i) j -> p c j i", i=4),
                w_raw[h][:].rearrange("p j (c i) -> p c j i", i=4),
                ACT.Copy,
            )
            codes_tag = "scale_bytes" if h == 0 else "w_codes1"
            w_codes.append(keep.tile([P, P], U32, name=f"w_codes{h}", tag=codes_tag, align_bytes=64))
            w_scales.append(keep.tile([P, P], U8, name=f"w_scales{h}", align_bytes=64))
            nc.vector.quantize_mx(w_codes[h][:].bitcast(FP8X4), w_scales[h][:], w_grouped[:].rearrange("p n j -> p (n j)"))

        knee_cols = keep.tile([P, HALVES], F32, name="knee_cols")
        nc.scalar.activation(knee_cols[:], bias_cols[:], ACT.Copy, bias=-KNEE, scale=-1.0)

        words = []
        for b in range(S // WIDE):
            words_tag = "grouped_bytes1" if b == 1 else "words0"
            words.append(keep.tile([P, WIDE], U32, name=f"words{b}", tag=words_tag, align_bytes=64))
            for c in range(0, WIDE, SLICE):
                first = b * WIDE + c
                entries = offsets[:, first // LIST_ROWS : (first + SLICE) // LIST_ROWS]
                nc.vector.tensor_copy(words[b][:, c : c + SLICE], word_table[:].bitcast(U32).indirect(entries))

        prob, goal_y, linear, miss = (unit_tiles(kind) for kind in ("prob", "goal_y", "linear", "miss"))
        slices = [(b, slice(c, c + SLICE)) for b in range(S // WIDE) for c in range(0, WIDE, SLICE)]
        sums = {}
        for b, cols in slices:
            for h in range(HALVES):
                sums[h, b, cols.start] = psum.tile([P, SLICE], F32, name=f"sums{h}{b}{cols.start}")
                nc.tensor.matmul_mx(
                    sums[h, b, cols.start][:],
                    lhsT=w_codes[h][:].bitcast(FP8X4),
                    lhsT_scale=w_scales[h][:],
                    rhs=words[b][:, cols].bitcast(FP8X4),
                    rhs_scale=scales[:, b * WIDE + cols.start : b * WIDE + cols.stop],
                    start=True,
                    stop=True,
                )
                nc.scalar.activation(prob[h, b][:, cols], sums[h, b, cols.start][:], ACT.Sigmoid, bias=bias_cols[:, h : h + 1])

        for b, cols in slices:
            for h in range(HALVES):
                nc.vector.scalar_tensor_tensor(
                    goal_y[h, b][:, cols], sums[h, b, cols.start][:], bias_cols[:, h : h + 1], goals[h, b][:, cols], ALU.add, ALU.mult
                )
            for h in range(HALVES):
                nc.vector.scalar_tensor_tensor(
                    linear[h, b][:, cols], sums[h, b, cols.start][:], knee_cols[:, h : h + 1], goal_y[h, b][:, cols], ALU.max, ALU.subtract
                )

        first_unit = [(units[0], slice(c, c + SLICE)) for c in range(0, WIDE, SLICE)]
        for u, cols in first_unit + [(u, slice(0, WIDE)) for u in units[1:-1]] + [(last, slice(0, GPSIMD_LAST))]:
            nc.gpsimd.tensor_tensor(miss[u][:, cols], goals[u][:, cols], prob[u][:, cols], ALU.subtract)
        nc.vector.tensor_tensor(miss[last][:, GPSIMD_LAST:], goals[last][:, GPSIMD_LAST:], prob[last][:, GPSIMD_LAST:], ALU.subtract)

        log_prob, weight, ce_less_bias = (unit_tiles(kind) for kind in ("log_prob", "weight", "ce_less_bias"))

        def cross_entropy(u, cols):
            if cols.start == 0:
                nc.scalar.activation(log_prob[u][:], prob[u][:], ACT.Ln, bias=floor[:])
            nc.vector.scalar_tensor_tensor(
                ce_less_bias[u][:, cols], log_prob[u][:, cols], -KNEE, linear[u][:, cols], ALU.max, ALU.subtract, reverse1=True
            )

        def loss(u, cols):
            h, b = u
            if cols.start == 0:
                nc.scalar.activation(weight[u][:], miss[u][:], ACT.Square)
            result = keep.tile([P, cols.stop - cols.start], F32, name=f"result{h}{b}{cols.start}")
            nc.vector.scalar_tensor_tensor(
                result[:], ce_less_bias[u][:, cols], bias_cols[:, h : h + 1], weight[u][:, cols], ALU.add, ALU.mult
            )
            nc.sync.dma_start(out[h * P : (h + 1) * P, b * WIDE + cols.start : b * WIDE + cols.stop], result[:])

        pieces = [(u, slice(0, WIDE)) for u in units[:-1]] + [(last, slice(c, c + SLICE)) for c in range(0, WIDE, SLICE)]
        cross_entropy(*pieces[0])
        for ahead, behind in zip(pieces[1:], pieces):
            cross_entropy(*ahead)
            loss(*behind)
        loss(*pieces[-1])
